import numpy as np
import ml_dtypes


def mxq(x, axis, fmt="e4m3"):
    dtype, down = {"e4m3": (ml_dtypes.float8_e4m3fn, 7), "e5m2": (ml_dtypes.float8_e5m2, 14)}[fmt]
    v = np.moveaxis(np.asarray(x, np.float32).astype(ml_dtypes.bfloat16).astype(np.float64), axis, -1)
    blocks = v.reshape(v.shape[:-1] + (-1, 32))
    amax = np.abs(blocks).max(-1, keepdims=True)
    byte = np.maximum(np.where(amax > 0, np.frexp(amax)[1] - 1 + 127, 0) - down, 1)
    scale = np.exp2(byte - 127.0)
    codes = (blocks / scale).astype(np.float32).astype(dtype).astype(np.float64)
    return np.moveaxis((codes * scale).reshape(v.shape), -1, axis)


WIDE = False


def mx_kscale(k):
    if not WIDE:
        return np.ones(k)
    levels = np.array([10, -10, 5, -5, 0])
    if k % 512:
        return np.exp2(np.random.permutation(np.resize(levels, k // 32))).repeat(32)
    a = np.empty((k // 512, 16))
    for p in range(k // 512):
        a[p, :8] = np.random.permutation(np.resize(levels, 8))
        for g in range(8):
            far = levels[np.abs(levels - a[p, g]) >= 10]
            a[p, g + 8] = far[np.random.randint(len(far))]
    return np.exp2(a.ravel()).repeat(32)


def f64(x):
    return np.asarray(x).astype(np.float64)


def striped(idx):
    return np.tile(idx.reshape(-1, 16).T, (8, 1)).astype(np.uint16)


def unstriped(offs):
    return offs[:16].T.reshape(-1).astype(np.int64)


def silu(v):
    return v / (1.0 + np.exp(-np.maximum(v, -700.0)))


K, T, E, C, N = 512, 1024, 8, 128, 512


def by_expert(wq, xq):
    return np.concatenate([wq[e].T @ xq[:, e * C:(e + 1) * C] for e in range(E)], axis=1)


def setup_inputs():
    n = np.random.standard_normal
    s = mx_kscale(K)[:, None]
    return {
        "xT": (n((K, T)) * s).astype(np.float32),
        "w": (n((E, K, N)) / np.sqrt(K) / s[None]).astype(np.float32),
        "b": (0.3 * n((N, E))).astype(np.float32),
        "gate": np.tile(np.random.uniform(0.2, 1.0, E * C), (N, 1)).astype(np.float32),
        "offs": striped(np.random.permutation(T)[:E * C]),
    }


def reference(xT, w, b, gate, offs):
    idx = unstriped(offs)
    xq = mxq(f64(xT)[:, idx], 0, "e4m3")
    y = by_expert(mxq(f64(w), 1, "e4m3"), xq)
    y = silu(y + np.repeat(f64(b), C, axis=1))
    out = np.zeros((N, T))
    out[:, idx] = f64(gate) * y
    return out

@@ -1,0 +1,132 @@
+from contextlib import ExitStack
+
+import concourse.mybir as mybir
+
+K, T, E, C, N = 512, 1024, 8, 128, 512
+FLOPS = 2 * K * N * E * C
+BYTES = 4 * (K * T + E * K * N + N * E + E * C + N * T) + 2 * 128 * (E * C // 16)
+
+F32 = mybir.dt.float32
+BF16 = mybir.dt.bfloat16
+U32 = mybir.dt.uint32
+U16 = mybir.dt.uint16
+U8 = mybir.dt.uint8
+FP8X4 = mybir.dt.float8_e4m3fn_x4
+SILU = mybir.ActivationFunctionType.Silu
+MULT = mybir.AluOpType.mult
+
+P = 128
+BLOCKS = N // P
+CHUNK = 512
+V_TOK = 320
+V_COLS = (256, 0, 0, 0, 0, 0, 0, 0)
+GROUPS = ((0,), (1,), (2, 3), (4, 5), (6, 7))
+GATHERS = ((0, 256), (256, 1024), None, None, None)
+
+
+def interleave(copy, grouped, raw, lo, hi):
+    copy(
+        out=grouped[:, lo:hi, :].rearrange("p (c i) t -> p c t i", i=4),
+        in_=raw[:, :, lo:hi].rearrange("p t (c i) -> p c t i", i=4),
+    )
+
+
+def tile_routed_moe_kernel(tc, xT, w, b, gate, offs, out):
+    nc = tc.nc
+    with ExitStack() as ctx:
+        keep = ctx.enter_context(tc.tile_pool(name="keep", bufs=1))
+        w_pool = ctx.enter_context(tc.tile_pool(name="w_pool", bufs=8))
+        x_pool = ctx.enter_context(tc.tile_pool(name="x_pool", bufs=2))
+        g_pool = ctx.enter_context(tc.tile_pool(name="g_pool", bufs=3))
+        q_pool = ctx.enter_context(tc.tile_pool(name="q_pool", bufs=3))
+        y_pool = ctx.enter_context(tc.tile_pool(name="y_pool", bufs=3))
+        psum = ctx.enter_context(tc.psum_pool(name="psum", bufs=4))
+
+        offsets = keep.tile([P, E * C // 16], U16, name="offsets")
+        nc.sync.dma_start(offsets[:], offs)
+
+        warm = keep.tile([P, 1], F32, name="warm")
+        warm_out = keep.tile([P, 1], F32, name="warm_out")
+        nc.gpsimd.memset(warm[:], 0.0)
+        nc.scalar.activation(warm_out[:], warm[:], SILU)
+
+        x_codes = keep.tile([P, T], U32, name="x_codes", align_bytes=64)
+        x_scales = keep.tile([P, T], U8, name="x_scales", align_bytes=64)
+        nc.gpsimd.memset(x_scales[:], 0)
+
+        bias = keep.tile([P, BLOCKS, E], F32, name="bias")
+        nc.scalar.dma_start(bias[:], b.rearrange("(m p) e -> p m e", p=P))
+
+        x_raws = []
+        for lo in range(0, T, CHUNK):
+            x_raw = x_pool.tile([P, 4, CHUNK], F32, name="x_raw")
+            nc.sync.dma_start(x_raw[:], xT[:, lo : lo + CHUNK].rearrange("(p t) c -> p t c", t=4))
+            x_raws.append(x_raw)
+
+        gates = keep.tile([P, E * C], F32, name="gates")
+        w_raws = []
+        for e in range(E):
+            w_raw = w_pool.tile([P, 4, N], F32, name="w_raw")
+            nc.sync.dma_start(w_raw[:], w[e].rearrange("(p t) n -> p t n", t=4))
+            w_raws.append(w_raw)
+            if e == 0:
+                nc.sync.dma_start(gates[:], gate[0:P, :])
+
+        for i, x_raw in enumerate(x_raws):
+            x_grouped = x_pool.tile([P, CHUNK, 4], BF16, name="x_grouped", align_bytes=64)
+            interleave(nc.vector.tensor_copy, x_grouped, x_raw, 0, V_TOK)
+            interleave(nc.scalar.copy, x_grouped, x_raw, V_TOK, CHUNK)
+            cols = slice(i * CHUNK, (i + 1) * CHUNK)
+            nc.vector.quantize_mx(
+                out=x_codes[:, cols].bitcast(FP8X4),
+                scales=x_scales[:, cols],
+                in_=x_grouped[:].rearrange("p c t -> p (c t)"),
+            )
+
+        g_codes = keep.tile([P, E * C], U32, name="g_codes", align_bytes=64)
+        g_scales = keep.tile([P, E * C], U8, name="g_scales", align_bytes=64)
+        results = [keep.tile([P, T], F32, name=f"result{m}") for m in range(BLOCKS)]
+        for piece, group in zip(GATHERS, GROUPS):
+            if piece:
+                cols = slice(*piece)
+                entries = offsets[:, piece[0] // 16 : piece[1] // 16]
+                nc.vector.tensor_copy(g_codes[:, cols], x_codes[:].indirect(entries))
+                nc.vector.tensor_copy(g_scales[:, cols], x_scales[:].indirect(entries))
+            width = len(group) * C
+            y = y_pool.tile([P, BLOCKS, width], F32, name="y")
+            for i, e in enumerate(group):
+                w_grouped = g_pool.tile([P, N, 4], BF16, name="w_grouped", align_bytes=64)
+                if V_COLS[e] > 0:
+                    interleave(nc.vector.tensor_copy, w_grouped, w_raws[e], 0, V_COLS[e])
+                interleave(nc.scalar.copy, w_grouped, w_raws[e], V_COLS[e], N)
+                w_codes = q_pool.tile([P, N], U32, name="w_codes", align_bytes=64)
+                w_scales = q_pool.tile([P, N], U8, name="w_scales", align_bytes=64)
+                nc.vector.quantize_mx(
+                    out=w_codes[:].bitcast(FP8X4),
+                    scales=w_scales[:],
+                    in_=w_grouped[:].rearrange("p c t -> p (c t)"),
+                )
+                sums = psum.tile([P, BLOCKS, C], F32, name="sums")
+                slots = slice(e * C, (e + 1) * C)
+                for m in range(BLOCKS):
+                    feats = slice(m * P, (m + 1) * P)
+                    nc.tensor.matmul_mx(
+                        out=sums[:, m, :],
+                        lhsT=w_codes[:, feats].bitcast(FP8X4),
+                        lhsT_scale=w_scales[:, feats],
+                        rhs=g_codes[:, slots].bitcast(FP8X4),
+                        rhs_scale=g_scales[:, slots],
+                        start=True,
+                        stop=True,
+                    )
+                for m in range(BLOCKS):
+                    nc.scalar.activation(
+                        y[:, m, i * C : (i + 1) * C], sums[:, m, :], SILU, bias=bias[:, m, e : e + 1]
+                    )
+            lo = group[0] * C
+            entries = offsets[:, lo // 16 : (lo + width) // 16]
+            for m in range(BLOCKS):
+                nc.vector.tensor_tensor(y[:, m, :], y[:, m, :], gates[:, lo : lo + width], MULT)
+                nc.vector.tensor_copy(results[m][:].indirect(entries), y[:, m, :])
+                if group == GROUPS[-1]:
+                    nc.sync.dma_start(out[m * P : (m + 1) * P, :], results[m][:])

@@ -126,7 +126,8 @@ def tile_routed_moe_kernel(tc, xT, w, b, gate, offs, out):
             lo = group[0] * C
             entries = offsets[:, lo // 16 : (lo + width) // 16]
             for m in range(BLOCKS):
-                nc.vector.tensor_tensor(y[:, m, :], y[:, m, :], gates[:, lo : lo + width], MULT)
-                nc.vector.tensor_copy(results[m][:].indirect(entries), y[:, m, :])
+                nc.vector.tensor_tensor(
+                    results[m][:].indirect(entries), y[:, m, :], gates[:, lo : lo + width], MULT
+                )
                 if group == GROUPS[-1]:
                     nc.sync.dma_start(out[m * P : (m + 1) * P, :], results[m][:])

@@ -17,11 +17,13 @@ MULT = mybir.AluOpType.mult
 
 P = 128
 BLOCKS = N // P
-CHUNK = 512
-V_TOK = 320
-V_COLS = (256, 0, 0, 0, 0, 0, 0, 0)
+CHUNKS = ((0, 512, 320), (512, 768, 160), (768, 1024, 160))
+V_COLS = (160, 0, 0, 0, 0, 0, 0, 0)
 GROUPS = ((0,), (1,), (2, 3), (4, 5), (6, 7))
-GATHERS = ((0, 256), (256, 1024), None, None, None)
+FIRST = 256
+HEAD = (0, 1)
+TAIL = (2, 3)
+S_STEP = 256
 
 
 def interleave(copy, grouped, raw, lo, hi):
@@ -36,15 +38,14 @@ def tile_routed_moe_kernel(tc, xT, w, b, gate, offs, out):
     with ExitStack() as ctx:
         keep = ctx.enter_context(tc.tile_pool(name="keep", bufs=1))
         w_pool = ctx.enter_context(tc.tile_pool(name="w_pool", bufs=8))
-        x_pool = ctx.enter_context(tc.tile_pool(name="x_pool", bufs=2))
+        x_pool = ctx.enter_context(tc.tile_pool(name="x_pool", bufs=3))
+        turn_pool = ctx.enter_context(tc.tile_pool(name="turn_pool", bufs=1))
         g_pool = ctx.enter_context(tc.tile_pool(name="g_pool", bufs=3))
         q_pool = ctx.enter_context(tc.tile_pool(name="q_pool", bufs=3))
         y_pool = ctx.enter_context(tc.tile_pool(name="y_pool", bufs=3))
-        psum = ctx.enter_context(tc.psum_pool(name="psum", bufs=4))
+        psum = ctx.enter_context(tc.psum_pool(name="psum", bufs=8))
 
         offsets = keep.tile([P, E * C // 16], U16, name="offsets")
-        nc.sync.dma_start(offsets[:], offs)
-
         warm = keep.tile([P, 1], F32, name="warm")
         warm_out = keep.tile([P, 1], F32, name="warm_out")
         nc.gpsimd.memset(warm[:], 0.0)
@@ -55,79 +56,122 @@ def tile_routed_moe_kernel(tc, xT, w, b, gate, offs, out):
         nc.gpsimd.memset(x_scales[:], 0)
 
         bias = keep.tile([P, BLOCKS, E], F32, name="bias")
-        nc.scalar.dma_start(bias[:], b.rearrange("(m p) e -> p m e", p=P))
+        gates = keep.tile([P, E * C], F32, name="gates")
 
         x_raws = []
-        for lo in range(0, T, CHUNK):
-            x_raw = x_pool.tile([P, 4, CHUNK], F32, name="x_raw")
-            nc.sync.dma_start(x_raw[:], xT[:, lo : lo + CHUNK].rearrange("(p t) c -> p t c", t=4))
+        for i, (lo, hi, share) in enumerate(CHUNKS):
+            x_raw = x_pool.tile([P, 4, hi - lo], F32, name="x_raw")
+            nc.sync.dma_start(x_raw[:], xT[:, lo:hi].rearrange("(p t) c -> p t c", t=4))
             x_raws.append(x_raw)
+            if i == 0:
+                nc.sync.dma_start(offsets[:], offs)
 
-        gates = keep.tile([P, E * C], F32, name="gates")
         w_raws = []
         for e in range(E):
             w_raw = w_pool.tile([P, 4, N], F32, name="w_raw")
             nc.sync.dma_start(w_raw[:], w[e].rearrange("(p t) n -> p t n", t=4))
             w_raws.append(w_raw)
             if e == 0:
+                nc.sync.dma_start(bias[:], b.rearrange("(m p) e -> p m e", p=P))
+            if e == 1:
                 nc.sync.dma_start(gates[:], gate[0:P, :])
 
-        for i, x_raw in enumerate(x_raws):
-            x_grouped = x_pool.tile([P, CHUNK, 4], BF16, name="x_grouped", align_bytes=64)
-            interleave(nc.vector.tensor_copy, x_grouped, x_raw, 0, V_TOK)
-            interleave(nc.scalar.copy, x_grouped, x_raw, V_TOK, CHUNK)
-            cols = slice(i * CHUNK, (i + 1) * CHUNK)
+        for (lo, hi, share), x_raw in zip(CHUNKS, x_raws):
+            x_grouped = x_pool.tile([P, hi - lo, 4], BF16, name="x_grouped", align_bytes=64)
+            interleave(nc.vector.tensor_copy, x_grouped, x_raw, 0, share)
+            interleave(nc.scalar.copy, x_grouped, x_raw, share, hi - lo)
             nc.vector.quantize_mx(
-                out=x_codes[:, cols].bitcast(FP8X4),
-                scales=x_scales[:, cols],
+                out=x_codes[:, lo:hi].bitcast(FP8X4),
+                scales=x_scales[:, lo:hi],
                 in_=x_grouped[:].rearrange("p c t -> p (c t)"),
             )
 
-        g_codes = keep.tile([P, E * C], U32, name="g_codes", align_bytes=64)
+        g_first = keep.tile([P, FIRST], U32, name="g_first", align_bytes=64)
         g_scales = keep.tile([P, E * C], U8, name="g_scales", align_bytes=64)
         results = [keep.tile([P, T], F32, name=f"result{m}") for m in range(BLOCKS)]
-        for piece, group in zip(GATHERS, GROUPS):
-            if piece:
-                cols = slice(*piece)
-                entries = offsets[:, piece[0] // 16 : piece[1] // 16]
-                nc.vector.tensor_copy(g_codes[:, cols], x_codes[:].indirect(entries))
-                nc.vector.tensor_copy(g_scales[:, cols], x_scales[:].indirect(entries))
-            width = len(group) * C
-            y = y_pool.tile([P, BLOCKS, width], F32, name="y")
-            for i, e in enumerate(group):
+
+        nc.vector.tensor_copy(g_first[:], x_codes[:].indirect(offsets[:, : FIRST // 16]))
+        nc.vector.tensor_copy(g_scales[:, :FIRST], x_scales[:].indirect(offsets[:, : FIRST // 16]))
+        g_codes = [g_first]
+
+        def lay_out(e):
+            if e == 0:
+                w_grouped = turn_pool.tile([P, N, 4], BF16, name="turn", align_bytes=64)
+            else:
                 w_grouped = g_pool.tile([P, N, 4], BF16, name="w_grouped", align_bytes=64)
-                if V_COLS[e] > 0:
-                    interleave(nc.vector.tensor_copy, w_grouped, w_raws[e], 0, V_COLS[e])
-                interleave(nc.scalar.copy, w_grouped, w_raws[e], V_COLS[e], N)
-                w_codes = q_pool.tile([P, N], U32, name="w_codes", align_bytes=64)
-                w_scales = q_pool.tile([P, N], U8, name="w_scales", align_bytes=64)
-                nc.vector.quantize_mx(
-                    out=w_codes[:].bitcast(FP8X4),
-                    scales=w_scales[:],
-                    in_=w_grouped[:].rearrange("p c t -> p (c t)"),
-                )
-                sums = psum.tile([P, BLOCKS, C], F32, name="sums")
-                slots = slice(e * C, (e + 1) * C)
-                for m in range(BLOCKS):
-                    feats = slice(m * P, (m + 1) * P)
-                    nc.tensor.matmul_mx(
-                        out=sums[:, m, :],
-                        lhsT=w_codes[:, feats].bitcast(FP8X4),
-                        lhsT_scale=w_scales[:, feats],
-                        rhs=g_codes[:, slots].bitcast(FP8X4),
-                        rhs_scale=g_scales[:, slots],
-                        start=True,
-                        stop=True,
-                    )
-                for m in range(BLOCKS):
-                    nc.scalar.activation(
-                        y[:, m, i * C : (i + 1) * C], sums[:, m, :], SILU, bias=bias[:, m, e : e + 1]
-                    )
-            lo = group[0] * C
-            entries = offsets[:, lo // 16 : (lo + width) // 16]
+            if V_COLS[e] > 0:
+                interleave(nc.vector.tensor_copy, w_grouped, w_raws[e], 0, V_COLS[e])
+            for lo in range(V_COLS[e], N, S_STEP):
+                interleave(nc.scalar.copy, w_grouped, w_raws[e], lo, min(N, lo + S_STEP))
+            return w_grouped
+
+        def quantize(w_grouped):
+            w_codes = q_pool.tile([P, N], U32, name="w_codes", align_bytes=64)
+            w_scales = q_pool.tile([P, N], U8, name="w_scales", align_bytes=64)
+            nc.vector.quantize_mx(
+                out=w_codes[:].bitcast(FP8X4),
+                scales=w_scales[:],
+                in_=w_grouped[:].rearrange("p c t -> p (c t)"),
+            )
+            return w_codes, w_scales
+
+        def multiply(e, w_codes, w_scales):
+            sums = psum.tile([P, BLOCKS, C], F32, name="sums")
+            slots = slice(e * C, (e + 1) * C)
+            if e * C < FIRST:
+                words = g_codes[0][:, slots]
+            else:
+                words = g_codes[1][:, e * C - FIRST : (e + 1) * C - FIRST]
             for m in range(BLOCKS):
+                feats = slice(m * P, (m + 1) * P)
+                nc.tensor.matmul_mx(
+                    out=sums[:, m, :],
+                    lhsT=w_codes[:, feats].bitcast(FP8X4),
+                    lhsT_scale=w_scales[:, feats],
+                    rhs=words.bitcast(FP8X4),
+                    rhs_scale=g_scales[:, slots],
+                    start=True,
+                    stop=True,
+                )
+            return sums
+
+        def activate(unit, blocks):
+            group, sums, y = unit
+            for m in blocks:
+                for place, e in enumerate(group):
+                    nc.scalar.activation(
+                        y[:, m, place * C : (place + 1) * C], sums[place][:, m, :], SILU, bias=bias[:, m, e : e + 1]
+                    )
+
+        def scatter(unit, blocks):
+            group, sums, y = unit
+            lo, width = group[0] * C, len(group) * C
+            entries = offsets[:, lo // 16 : (lo + width) // 16]
+            for m in blocks:
                 nc.vector.tensor_tensor(
                     results[m][:].indirect(entries), y[:, m, :], gates[:, lo : lo + width], MULT
                 )
                 if group == GROUPS[-1]:
                     nc.sync.dma_start(out[m * P : (m + 1) * P, :], results[m][:])
+
+        last = None
+        for group in GROUPS:
+            grouped = [lay_out(e) for e in group]
+            if last:
+                activate(last, TAIL)
+            quantized = [quantize(g) for g in grouped]
+            if group == GROUPS[0]:
+                nc.vector.tensor_copy(g_scales[:, FIRST:], x_scales[:].indirect(offsets[:, FIRST // 16 :]))
+                g_rest = turn_pool.tile([P, E * C - FIRST], U32, name="turn", align_bytes=64)
+                nc.vector.tensor_copy(g_rest[:], x_codes[:].indirect(offsets[:, FIRST // 16 :]))
+                g_codes.append(g_rest)
+            sums = [multiply(e, *codes) for e, codes in zip(group, quantized)]
+            y = y_pool.tile([P, BLOCKS, len(group) * C], F32, name="y")
+            unit = (group, sums, y)
+            activate(unit, HEAD)
+            if last:
+                scatter(last, TAIL)
+            scatter(unit, HEAD)
+            last = unit
+        activate(last, TAIL)
+        scatter(last, TAIL)

@@ -18,9 +18,9 @@ MULT = mybir.AluOpType.mult
 P = 128
 BLOCKS = N // P
 CHUNKS = ((0, 512, 320), (512, 768, 160), (768, 1024, 160))
-V_COLS = (160, 0, 0, 0, 0, 0, 0, 0)
-GROUPS = ((0,), (1,), (2, 3), (4, 5), (6, 7))
-FIRST = 256
+V_COLS = (0, 0, 0, 0, 0, 0, 0, 0)
+GROUPS = ((0,), (1,), (2,), (3,), (4, 5), (6, 7))
+FIRST = 384
 HEAD = (0, 1)
 TAIL = (2, 3)
 S_STEP = 256

@@ -3,8 +3,10 @@ from contextlib import ExitStack
 import concourse.mybir as mybir
 
 K, T, E, C, N = 512, 1024, 8, 128, 512
-FLOPS = 2 * K * N * E * C
-BYTES = 4 * (K * T + E * K * N + N * E + E * C + N * T) + 2 * 128 * (E * C // 16)
+SLOTS = E * C
+
+FLOPS = 2 * K * N * SLOTS
+BYTES = 4 * (K * T + E * K * N + N * E + SLOTS + N * T) + 2 * 128 * (SLOTS // 16)
 
 F32 = mybir.dt.float32
 BF16 = mybir.dt.bfloat16
@@ -16,20 +18,34 @@ SILU = mybir.ActivationFunctionType.Silu
 MULT = mybir.AluOpType.mult
 
 P = 128
-BLOCKS = N // P
-CHUNKS = ((0, 512, 320), (512, 768, 160), (768, 1024, 160))
-V_COLS = (0, 0, 0, 0, 0, 0, 0, 0)
-GROUPS = ((0,), (1,), (2,), (3,), (4, 5), (6, 7))
-FIRST = 384
-HEAD = (0, 1)
-TAIL = (2, 3)
-S_STEP = 256
+PACK = 4
+RUN = 4
+BANDS = N // P
+PER_COLUMN = 16
+
+PIECES = ((0, 512), (512, 768), (768, 1024))
+VECTOR_COLUMNS = {512: 320, 256: 160}
+WEIGHT_COLUMNS = 256
+
+EARLY = 3 * C
+
+UNITS = ((0,), (1,), (2,), (3,), (4, 5), (6, 7))
+HALVES = ((0, 1), (2, 3))
+HALVES_AFTER = (1, 1, 1, 2, 1, 1, 2, 3)
 
 
-def interleave(copy, grouped, raw, lo, hi):
+def interleave(copy, grouped, raw, first, end):
     copy(
-        out=grouped[:, lo:hi, :].rearrange("p (c i) t -> p c t i", i=4),
-        in_=raw[:, :, lo:hi].rearrange("p t (c i) -> p c t i", i=4),
+        out=grouped[:, first:end, :].rearrange("p (c i) t -> p c t i", i=RUN),
+        in_=raw[:, :, first:end].rearrange("p t (c i) -> p c t i", i=RUN),
+    )
+
+
+def quantize(nc, codes, scales, grouped):
+    nc.vector.quantize_mx(
+        out=codes.bitcast(FP8X4),
+        scales=scales,
+        in_=grouped[:].rearrange("p c t -> p (c t)"),
     )
 
 
@@ -37,141 +53,125 @@ def tile_routed_moe_kernel(tc, xT, w, b, gate, offs, out):
     nc = tc.nc
     with ExitStack() as ctx:
         keep = ctx.enter_context(tc.tile_pool(name="keep", bufs=1))
-        w_pool = ctx.enter_context(tc.tile_pool(name="w_pool", bufs=8))
-        x_pool = ctx.enter_context(tc.tile_pool(name="x_pool", bufs=3))
+        w_pool = ctx.enter_context(tc.tile_pool(name="w_pool", bufs=E))
+        x_pool = ctx.enter_context(tc.tile_pool(name="x_pool", bufs=len(PIECES)))
         turn_pool = ctx.enter_context(tc.tile_pool(name="turn_pool", bufs=1))
-        g_pool = ctx.enter_context(tc.tile_pool(name="g_pool", bufs=3))
-        q_pool = ctx.enter_context(tc.tile_pool(name="q_pool", bufs=3))
-        y_pool = ctx.enter_context(tc.tile_pool(name="y_pool", bufs=3))
+        grouped_pool = ctx.enter_context(tc.tile_pool(name="grouped_pool", bufs=4))
+        codes_pool = ctx.enter_context(tc.tile_pool(name="codes_pool", bufs=4))
+        y_pool = ctx.enter_context(tc.tile_pool(name="y_pool", bufs=1))
         psum = ctx.enter_context(tc.psum_pool(name="psum", bufs=8))
 
-        offsets = keep.tile([P, E * C // 16], U16, name="offsets")
-        warm = keep.tile([P, 1], F32, name="warm")
-        warm_out = keep.tile([P, 1], F32, name="warm_out")
-        nc.gpsimd.memset(warm[:], 0.0)
-        nc.scalar.activation(warm_out[:], warm[:], SILU)
+        offsets = keep.tile([P, SLOTS // PER_COLUMN], U16, name="offsets")
+
+        zero = keep.tile([P, 1], F32, name="zero")
+        unused = keep.tile([P, 1], F32, name="unused")
+        nc.gpsimd.memset(zero[:], 0.0)
+        nc.scalar.activation(unused[:], zero[:], SILU)
 
         x_codes = keep.tile([P, T], U32, name="x_codes", align_bytes=64)
         x_scales = keep.tile([P, T], U8, name="x_scales", align_bytes=64)
         nc.gpsimd.memset(x_scales[:], 0)
 
-        bias = keep.tile([P, BLOCKS, E], F32, name="bias")
-        gates = keep.tile([P, E * C], F32, name="gates")
+        bias = keep.tile([P, BANDS, E], F32, name="bias")
+        gates = keep.tile([P, SLOTS], F32, name="gates")
 
         x_raws = []
-        for i, (lo, hi, share) in enumerate(CHUNKS):
-            x_raw = x_pool.tile([P, 4, hi - lo], F32, name="x_raw")
-            nc.sync.dma_start(x_raw[:], xT[:, lo:hi].rearrange("(p t) c -> p t c", t=4))
+        for i, (first, end) in enumerate(PIECES):
+            x_raw = x_pool.tile([P, PACK, end - first], F32, name="x_raw")
+            nc.sync.dma_start(x_raw[:], xT[:, first:end].rearrange("(p t) c -> p t c", t=PACK))
             x_raws.append(x_raw)
             if i == 0:
                 nc.sync.dma_start(offsets[:], offs)
-
         w_raws = []
         for e in range(E):
-            w_raw = w_pool.tile([P, 4, N], F32, name="w_raw")
-            nc.sync.dma_start(w_raw[:], w[e].rearrange("(p t) n -> p t n", t=4))
+            w_raw = w_pool.tile([P, PACK, N], F32, name="w_raw")
+            nc.sync.dma_start(w_raw[:], w[e].rearrange("(p t) n -> p t n", t=PACK))
             w_raws.append(w_raw)
             if e == 0:
                 nc.sync.dma_start(bias[:], b.rearrange("(m p) e -> p m e", p=P))
             if e == 1:
                 nc.sync.dma_start(gates[:], gate[0:P, :])
 
-        for (lo, hi, share), x_raw in zip(CHUNKS, x_raws):
-            x_grouped = x_pool.tile([P, hi - lo, 4], BF16, name="x_grouped", align_bytes=64)
-            interleave(nc.vector.tensor_copy, x_grouped, x_raw, 0, share)
-            interleave(nc.scalar.copy, x_grouped, x_raw, share, hi - lo)
-            nc.vector.quantize_mx(
-                out=x_codes[:, lo:hi].bitcast(FP8X4),
-                scales=x_scales[:, lo:hi],
-                in_=x_grouped[:].rearrange("p c t -> p (c t)"),
-            )
+        for (first, end), x_raw in zip(PIECES, x_raws):
+            width = end - first
+            x_grouped = x_pool.tile([P, width, PACK], BF16, name="x_grouped", align_bytes=64)
+            interleave(nc.vector.tensor_copy, x_grouped, x_raw, 0, VECTOR_COLUMNS[width])
+            interleave(nc.scalar.copy, x_grouped, x_raw, VECTOR_COLUMNS[width], width)
+            quantize(nc, x_codes[:, first:end], x_scales[:, first:end], x_grouped)
 
-        g_first = keep.tile([P, FIRST], U32, name="g_first", align_bytes=64)
-        g_scales = keep.tile([P, E * C], U8, name="g_scales", align_bytes=64)
-        results = [keep.tile([P, T], F32, name=f"result{m}") for m in range(BLOCKS)]
+        early = offsets[:, : EARLY // PER_COLUMN]
+        late = offsets[:, EARLY // PER_COLUMN :]
+        early_codes = keep.tile([P, EARLY], U32, name="early_codes", align_bytes=64)
+        slot_scales = keep.tile([P, SLOTS], U8, name="slot_scales", align_bytes=64)
+        results = [keep.tile([P, T], F32, name=f"result{m}") for m in range(BANDS)]
+        nc.vector.tensor_copy(early_codes[:], x_codes[:].indirect(early))
+        nc.vector.tensor_copy(slot_scales[:, :EARLY], x_scales[:].indirect(early))
 
-        nc.vector.tensor_copy(g_first[:], x_codes[:].indirect(offsets[:, : FIRST // 16]))
-        nc.vector.tensor_copy(g_scales[:, :FIRST], x_scales[:].indirect(offsets[:, : FIRST // 16]))
-        g_codes = [g_first]
-
-        def lay_out(e):
+        def quantize_weights(e):
             if e == 0:
-                w_grouped = turn_pool.tile([P, N, 4], BF16, name="turn", align_bytes=64)
+                w_grouped = turn_pool.tile([P, N, PACK], BF16, name="turn", align_bytes=64)
             else:
-                w_grouped = g_pool.tile([P, N, 4], BF16, name="w_grouped", align_bytes=64)
-            if V_COLS[e] > 0:
-                interleave(nc.vector.tensor_copy, w_grouped, w_raws[e], 0, V_COLS[e])
-            for lo in range(V_COLS[e], N, S_STEP):
-                interleave(nc.scalar.copy, w_grouped, w_raws[e], lo, min(N, lo + S_STEP))
-            return w_grouped
-
-        def quantize(w_grouped):
-            w_codes = q_pool.tile([P, N], U32, name="w_codes", align_bytes=64)
-            w_scales = q_pool.tile([P, N], U8, name="w_scales", align_bytes=64)
-            nc.vector.quantize_mx(
-                out=w_codes[:].bitcast(FP8X4),
-                scales=w_scales[:],
-                in_=w_grouped[:].rearrange("p c t -> p (c t)"),
-            )
+                w_grouped = grouped_pool.tile([P, N, PACK], BF16, name="w_grouped", align_bytes=64)
+            for first in range(0, N, WEIGHT_COLUMNS):
+                interleave(nc.scalar.copy, w_grouped, w_raws[e], first, first + WEIGHT_COLUMNS)
+            w_codes = codes_pool.tile([P, N], U32, name="w_codes", align_bytes=64)
+            w_scales = codes_pool.tile([P, N], U8, name="w_scales", align_bytes=64)
+            quantize(nc, w_codes[:], w_scales[:], w_grouped)
             return w_codes, w_scales
 
         def multiply(e, w_codes, w_scales):
-            sums = psum.tile([P, BLOCKS, C], F32, name="sums")
+            sums = psum.tile([P, BANDS, C], F32, name="sums")
             slots = slice(e * C, (e + 1) * C)
-            if e * C < FIRST:
-                words = g_codes[0][:, slots]
+            if e * C < EARLY:
+                words = early_codes[:, slots]
             else:
-                words = g_codes[1][:, e * C - FIRST : (e + 1) * C - FIRST]
-            for m in range(BLOCKS):
-                feats = slice(m * P, (m + 1) * P)
+                words = late_codes[:, e * C - EARLY : (e + 1) * C - EARLY]
+            for m in range(BANDS):
+                features = slice(m * P, (m + 1) * P)
                 nc.tensor.matmul_mx(
                     out=sums[:, m, :],
-                    lhsT=w_codes[:, feats].bitcast(FP8X4),
-                    lhsT_scale=w_scales[:, feats],
+                    lhsT=w_codes[:, features].bitcast(FP8X4),
+                    lhsT_scale=w_scales[:, features],
                     rhs=words.bitcast(FP8X4),
-                    rhs_scale=g_scales[:, slots],
+                    rhs_scale=slot_scales[:, slots],
                     start=True,
                     stop=True,
                 )
             return sums
 
-        def activate(unit, blocks):
-            group, sums, y = unit
-            for m in blocks:
-                for place, e in enumerate(group):
+        def finish(unit, bands):
+            experts, unit_sums, y = unit
+            for m in bands:
+                for place, e in enumerate(experts):
                     nc.scalar.activation(
-                        y[:, m, place * C : (place + 1) * C], sums[place][:, m, :], SILU, bias=bias[:, m, e : e + 1]
+                        y[:, m, place * C : (place + 1) * C],
+                        unit_sums[place][:, m, :],
+                        SILU,
+                        bias=bias[:, m, e : e + 1],
                     )
-
-        def scatter(unit, blocks):
-            group, sums, y = unit
-            lo, width = group[0] * C, len(group) * C
-            entries = offsets[:, lo // 16 : (lo + width) // 16]
-            for m in blocks:
-                nc.vector.tensor_tensor(
-                    results[m][:].indirect(entries), y[:, m, :], gates[:, lo : lo + width], MULT
-                )
-                if group == GROUPS[-1]:
+            first = experts[0] * C
+            end = first + len(experts) * C
+            entries = offsets[:, first // PER_COLUMN : end // PER_COLUMN]
+            for m in bands:
+                nc.vector.tensor_tensor(results[m][:].indirect(entries), y[:, m, :], gates[:, first:end], MULT)
+                if experts == UNITS[-1]:
                     nc.sync.dma_start(out[m * P : (m + 1) * P, :], results[m][:])
 
-        last = None
-        for group in GROUPS:
-            grouped = [lay_out(e) for e in group]
-            if last:
-                activate(last, TAIL)
-            quantized = [quantize(g) for g in grouped]
-            if group == GROUPS[0]:
-                nc.vector.tensor_copy(g_scales[:, FIRST:], x_scales[:].indirect(offsets[:, FIRST // 16 :]))
-                g_rest = turn_pool.tile([P, E * C - FIRST], U32, name="turn", align_bytes=64)
-                nc.vector.tensor_copy(g_rest[:], x_codes[:].indirect(offsets[:, FIRST // 16 :]))
-                g_codes.append(g_rest)
-            sums = [multiply(e, *codes) for e, codes in zip(group, quantized)]
-            y = y_pool.tile([P, BLOCKS, len(group) * C], F32, name="y")
-            unit = (group, sums, y)
-            activate(unit, HEAD)
-            if last:
-                scatter(last, TAIL)
-            scatter(unit, HEAD)
-            last = unit
-        activate(last, TAIL)
-        scatter(last, TAIL)
+        units = []
+        for experts in UNITS:
+            y = y_pool.tile([P, BANDS, len(experts) * C], F32, name=f"y{experts[0]}")
+            units.append((experts, [], y))
+        halves = [(unit, bands) for unit in units for bands in HALVES]
+
+        for e in range(E):
+            w_codes, w_scales = quantize_weights(e)
+            if e == 0:
+                nc.vector.tensor_copy(slot_scales[:, EARLY:], x_scales[:].indirect(late))
+                late_codes = turn_pool.tile([P, SLOTS - EARLY], U32, name="turn", align_bytes=64)
+                nc.vector.tensor_copy(late_codes[:], x_codes[:].indirect(late))
+            sums = multiply(e, w_codes, w_scales)
+            for experts, unit_sums, y in units:
+                if e in experts:
+                    unit_sums.append(sums)
+            for step in range(HALVES_AFTER[e]):
+                finish(*halves.pop(0))

from contextlib import ExitStack

import concourse.mybir as mybir

K, T, E, C, N = 512, 1024, 8, 128, 512
SLOTS = E * C

FLOPS = 2 * K * N * SLOTS
BYTES = 4 * (K * T + E * K * N + N * E + SLOTS + N * T) + 2 * 128 * (SLOTS // 16)

F32 = mybir.dt.float32
BF16 = mybir.dt.bfloat16
U32 = mybir.dt.uint32
U16 = mybir.dt.uint16
U8 = mybir.dt.uint8
FP8X4 = mybir.dt.float8_e4m3fn_x4
SILU = mybir.ActivationFunctionType.Silu
MULT = mybir.AluOpType.mult

P = 128
PACK = 4
RUN = 4
BANDS = N // P
PER_COLUMN = 16

PIECES = ((0, 512), (512, 768), (768, 1024))
VECTOR_COLUMNS = {512: 320, 256: 160}
WEIGHT_COLUMNS = 256

EARLY = 3 * C

UNITS = ((0,), (1,), (2,), (3,), (4, 5), (6, 7))
HALVES = ((0, 1), (2, 3))
HALVES_AFTER = (1, 1, 1, 2, 1, 1, 2, 3)


def interleave(copy, grouped, raw, first, end):
    copy(
        out=grouped[:, first:end, :].rearrange("p (c i) t -> p c t i", i=RUN),
        in_=raw[:, :, first:end].rearrange("p t (c i) -> p c t i", i=RUN),
    )


def quantize(nc, codes, scales, grouped):
    nc.vector.quantize_mx(
        out=codes.bitcast(FP8X4),
        scales=scales,
        in_=grouped[:].rearrange("p c t -> p (c t)"),
    )


def tile_routed_moe_kernel(tc, xT, w, b, gate, offs, out):
    nc = tc.nc
    with ExitStack() as ctx:
        keep = ctx.enter_context(tc.tile_pool(name="keep", bufs=1))
        w_pool = ctx.enter_context(tc.tile_pool(name="w_pool", bufs=E))
        x_pool = ctx.enter_context(tc.tile_pool(name="x_pool", bufs=len(PIECES)))
        turn_pool = ctx.enter_context(tc.tile_pool(name="turn_pool", bufs=1))
        grouped_pool = ctx.enter_context(tc.tile_pool(name="grouped_pool", bufs=4))
        codes_pool = ctx.enter_context(tc.tile_pool(name="codes_pool", bufs=4))
        y_pool = ctx.enter_context(tc.tile_pool(name="y_pool", bufs=1))
        psum = ctx.enter_context(tc.psum_pool(name="psum", bufs=8))

        offsets = keep.tile([P, SLOTS // PER_COLUMN], U16, name="offsets")

        zero = keep.tile([P, 1], F32, name="zero")
        unused = keep.tile([P, 1], F32, name="unused")
        nc.gpsimd.memset(zero[:], 0.0)
        nc.scalar.activation(unused[:], zero[:], SILU)

        x_codes = keep.tile([P, T], U32, name="x_codes", align_bytes=64)
        x_scales = keep.tile([P, T], U8, name="x_scales", align_bytes=64)
        nc.gpsimd.memset(x_scales[:], 0)

        bias = keep.tile([P, BANDS, E], F32, name="bias")
        gates = keep.tile([P, SLOTS], F32, name="gates")

        x_raws = []
        for i, (first, end) in enumerate(PIECES):
            x_raw = x_pool.tile([P, PACK, end - first], F32, name="x_raw")
            nc.sync.dma_start(x_raw[:], xT[:, first:end].rearrange("(p t) c -> p t c", t=PACK))
            x_raws.append(x_raw)
            if i == 0:
                nc.sync.dma_start(offsets[:], offs)
        w_raws = []
        for e in range(E):
            w_raw = w_pool.tile([P, PACK, N], F32, name="w_raw")
            nc.sync.dma_start(w_raw[:], w[e].rearrange("(p t) n -> p t n", t=PACK))
            w_raws.append(w_raw)
            if e == 0:
                nc.sync.dma_start(bias[:], b.rearrange("(m p) e -> p m e", p=P))
            if e == 1:
                nc.sync.dma_start(gates[:], gate[0:P, :])

        for (first, end), x_raw in zip(PIECES, x_raws):
            width = end - first
            x_grouped = x_pool.tile([P, width, PACK], BF16, name="x_grouped", align_bytes=64)
            interleave(nc.vector.tensor_copy, x_grouped, x_raw, 0, VECTOR_COLUMNS[width])
            interleave(nc.scalar.copy, x_grouped, x_raw, VECTOR_COLUMNS[width], width)
            quantize(nc, x_codes[:, first:end], x_scales[:, first:end], x_grouped)

        early = offsets[:, : EARLY // PER_COLUMN]
        late = offsets[:, EARLY // PER_COLUMN :]
        early_codes = keep.tile([P, EARLY], U32, name="early_codes", align_bytes=64)
        slot_scales = keep.tile([P, SLOTS], U8, name="slot_scales", align_bytes=64)
        results = [keep.tile([P, T], F32, name=f"result{m}") for m in range(BANDS)]
        nc.vector.tensor_copy(early_codes[:], x_codes[:].indirect(early))
        nc.vector.tensor_copy(slot_scales[:, :EARLY], x_scales[:].indirect(early))

        def quantize_weights(e):
            if e == 0:
                w_grouped = turn_pool.tile([P, N, PACK], BF16, name="turn", align_bytes=64)
            else:
                w_grouped = grouped_pool.tile([P, N, PACK], BF16, name="w_grouped", align_bytes=64)
            for first in range(0, N, WEIGHT_COLUMNS):
                interleave(nc.scalar.copy, w_grouped, w_raws[e], first, first + WEIGHT_COLUMNS)
            w_codes = codes_pool.tile([P, N], U32, name="w_codes", align_bytes=64)
            w_scales = codes_pool.tile([P, N], U8, name="w_scales", align_bytes=64)
            quantize(nc, w_codes[:], w_scales[:], w_grouped)
            return w_codes, w_scales

        def multiply(e, w_codes, w_scales):
            sums = psum.tile([P, BANDS, C], F32, name="sums")
            slots = slice(e * C, (e + 1) * C)
            if e * C < EARLY:
                words = early_codes[:, slots]
            else:
                words = late_codes[:, e * C - EARLY : (e + 1) * C - EARLY]
            for m in range(BANDS):
                features = slice(m * P, (m + 1) * P)
                nc.tensor.matmul_mx(
                    out=sums[:, m, :],
                    lhsT=w_codes[:, features].bitcast(FP8X4),
                    lhsT_scale=w_scales[:, features],
                    rhs=words.bitcast(FP8X4),
                    rhs_scale=slot_scales[:, slots],
                    start=True,
                    stop=True,
                )
            return sums

        def finish(unit, bands):
            experts, unit_sums, y = unit
            for m in bands:
                for place, e in enumerate(experts):
                    nc.scalar.activation(
                        y[:, m, place * C : (place + 1) * C],
                        unit_sums[place][:, m, :],
                        SILU,
                        bias=bias[:, m, e : e + 1],
                    )
            first = experts[0] * C
            end = first + len(experts) * C
            entries = offsets[:, first // PER_COLUMN : end // PER_COLUMN]
            for m in bands:
                nc.vector.tensor_tensor(results[m][:].indirect(entries), y[:, m, :], gates[:, first:end], MULT)
                if experts == UNITS[-1]:
                    nc.sync.dma_start(out[m * P : (m + 1) * P, :], results[m][:])

        units = []
        for experts in UNITS:
            y = y_pool.tile([P, BANDS, len(experts) * C], F32, name=f"y{experts[0]}")
            units.append((experts, [], y))
        halves = [(unit, bands) for unit in units for bands in HALVES]

        for e in range(E):
            w_codes, w_scales = quantize_weights(e)
            if e == 0:
                nc.vector.tensor_copy(slot_scales[:, EARLY:], x_scales[:].indirect(late))
                late_codes = turn_pool.tile([P, SLOTS - EARLY], U32, name="turn", align_bytes=64)
                nc.vector.tensor_copy(late_codes[:], x_codes[:].indirect(late))
            sums = multiply(e, w_codes, w_scales)
            for experts, unit_sums, y in units:
                if e in experts:
                    unit_sums.append(sums)
            for step in range(HALVES_AFTER[e]):
                finish(*halves.pop(0))
